import numpy as np
import ml_dtypes


def mxq(x, axis, fmt="e4m3"):
    dtype, down = {"e4m3": (ml_dtypes.float8_e4m3fn, 7), "e5m2": (ml_dtypes.float8_e5m2, 14)}[fmt]
    v = np.moveaxis(np.asarray(x, np.float32).astype(ml_dtypes.bfloat16).astype(np.float64), axis, -1)
    blocks = v.reshape(v.shape[:-1] + (-1, 32))
    amax = np.abs(blocks).max(-1, keepdims=True)
    byte = np.maximum(np.where(amax > 0, np.frexp(amax)[1] - 1 + 127, 0) - down, 1)
    scale = np.exp2(byte - 127.0)
    codes = (blocks / scale).astype(np.float32).astype(dtype).astype(np.float64)
    return np.moveaxis((codes * scale).reshape(v.shape), -1, axis)


WIDE = False


def mx_kscale(k):
    if not WIDE:
        return np.ones(k)
    levels = np.array([10, -10, 5, -5, 0])
    if k % 512:
        return np.exp2(np.random.permutation(np.resize(levels, k // 32))).repeat(32)
    a = np.empty((k // 512, 16))
    for p in range(k // 512):
        a[p, :8] = np.random.permutation(np.resize(levels, 8))
        for g in range(8):
            far = levels[np.abs(levels - a[p, g]) >= 10]
            a[p, g + 8] = far[np.random.randint(len(far))]
    return np.exp2(a.ravel()).repeat(32)


def f64(x):
    return np.asarray(x).astype(np.float64)


def striped(idx):
    return np.tile(np.asarray(idx).reshape(-1, 16).T, (8, 1)).astype(np.uint16)


def unstriped(offs):
    return offs[:16].T.reshape(-1).astype(np.int64)


def striped8(idx):
    return np.asarray(idx).reshape(8, -1, 16).transpose(0, 2, 1).reshape(128, -1).astype(np.uint16)


def unstriped8(offs):
    return offs.reshape(8, 16, -1).transpose(0, 2, 1).reshape(8, -1).astype(np.int64)


def pick8(x, idx, run):
    r = np.arange(len(x))
    return x[r[:, None], idx[r % (8 * run) // run]]


E2M1 = np.array([0.0, 0.5, 1.0, 1.5, 2.0, 3.0, 4.0, 6.0, -0.0, -0.5, -1.0, -1.5, -2.0, -3.0, -4.0, -6.0])


def pack_weight(w, fmt):
    k, n = w.shape
    w = f64(np.asarray(w, np.float32).astype(ml_dtypes.bfloat16)).reshape(k // 32, 32, n)
    amax = np.abs(w).max(1)
    if fmt == "e4m3":
        byte = np.frexp(amax)[1] - 1 + 127 - 7
    else:
        mant, ex = np.frexp(amax / 6.0)
        byte = np.where(mant > 0.5, ex, ex - 1) + 127
    byte = np.clip(np.where(amax > 0, byte, 1), 1, 254)
    scaled = (w * np.exp2(127.0 - byte)[:, None, :]).reshape(k, n).astype(np.float32)
    by_word = np.ascontiguousarray(scaled.reshape(k // 512, 128, 4, n).transpose(0, 1, 3, 2))
    if fmt == "e4m3":
        words = by_word.astype(ml_dtypes.float8_e4m3fn).view(np.uint8)
    else:
        c = by_word.astype(ml_dtypes.float4_e2m1fn).view(np.uint8) & 0xF
        words = (c[..., 0::2] | (c[..., 1::2] << 4)).reshape(k // 512, 128, 2 * n)
    return np.ascontiguousarray(words), np.ascontiguousarray(byte.astype(np.uint8).reshape(k // 512, 16, n))


def unpack_weight(words, scales, fmt):
    g, _, n = scales.shape
    words = np.ascontiguousarray(words).reshape(g, 128, n, -1)
    if fmt == "e4m3":
        vals = words.view(ml_dtypes.float8_e4m3fn).astype(np.float64)
    else:
        nib = np.empty((g, 128, n, 4), np.uint8)
        nib[..., 0::2] = words & 0xF
        nib[..., 1::2] = words >> 4
        vals = E2M1[nib]
    vals = vals * np.repeat(np.exp2(scales.astype(np.float64) - 127.0), 8, axis=1)[..., None]
    return vals.transpose(0, 1, 3, 2).reshape(g * 512, n)


def sigmoid(v):
    return 1.0 / (1.0 + np.exp(-v))


K, R, F, T, J, M, G = 512, 128, 512, 2048, 512, 256, 32


def setup_inputs():
    n = np.random.standard_normal
    idx = np.random.permutation(T)[:J]
    idx2 = np.stack([np.random.permutation(J)[:M] for _ in range(8)])
    fk = mx_kscale(K)
    ff = mx_kscale(F)
    tabp = pack_weight(n((K, T)) / fk[:, None], "e2m1")
    return {
        "tab_words": tabp[0],
        "tab_scales": tabp[1],
        "w1": (n((K, R)) * 1 / np.sqrt(K) * fk[:, None]).astype(np.float32),
        "gain": (np.random.uniform(0.5, 1.5, (R, 1))).astype(np.float32),
        "pb": (np.random.uniform(-0.7, 0.7, (1, M))).astype(np.float32),
        "wo": (n((F, R)) * 1 / np.sqrt(F) * ff[:, None]).astype(np.float32),
        "dy": (n((F, M)) / ff[:, None]).astype(np.float32),
        "old": (0.5 * n((R, J))).astype(np.float32),
        "offs": striped(idx),
        "offs2": striped8(idx2),
    }


def reference(tab_words, tab_scales, w1, gain, pb, wo, dy, old, offs, offs2):
    idx = unstriped(offs)
    idx2 = unstriped8(offs2)
    tabu = unpack_weight(tab_words, tab_scales, "e2m1")
    w1q = mxq(f64(w1), 0, "e4m3")
    tabidxg = tabu[:, idx]
    a = w1q.T @ tabidxg
    h1 = a * f64(gain)
    s = pick8(h1, idx2, 16) + f64(pb)
    q2 = np.sqrt(np.square(s).reshape(R, G, M // G).mean(axis=2) + 0.1)
    qr = np.repeat(q2, M // G, axis=1)
    woq = mxq(f64(wo), 0, "e4m3")
    dyq = mxq(f64(dy), 0, "e4m3")
    c0 = woq.T @ dyq
    dqr = c0 * sigmoid(s / qr) * (1.0 + s / qr * (1.0 - sigmoid(s / qr))) * s / np.square(qr) * (-1.0)
    dq2 = dqr.reshape(R, G, M // G).sum(axis=2)
    e1 = dq2 * 0.5 / np.sqrt(np.square(s).reshape(R, G, M // G).mean(axis=2) + 0.1) / 8.0
    r1 = np.repeat(e1, M // G, axis=1)
    ds = c0 * sigmoid(s / qr) * (1.0 + s / qr * (1.0 - sigmoid(s / qr))) / qr + r1 * s * 2.0
    s2 = np.zeros((R, J))
    s2[np.arange(R)[:, None], idx2[np.arange(R) % 128 // 16]] = ds
    da = s2 * f64(gain)
    y = da + f64(old)
    return y

@@ -1,0 +1,188 @@
+from contextlib import ExitStack
+
+import concourse.mybir as mybir
+from concourse.masks import make_identity
+
+K, R, F, T, J, M, G = 512, 128, 512, 2048, 512, 256, 32
+P = 128
+PACK = 4
+GROUP = M // G
+FLOPS = 2 * K * R * J + 2 * F * R * M
+
+F32 = mybir.dt.float32
+BF16 = mybir.dt.bfloat16
+I32 = mybir.dt.int32
+U32 = mybir.dt.uint32
+U16 = mybir.dt.uint16
+U8 = mybir.dt.uint8
+FP8X4 = mybir.dt.float8_e4m3fn_x4
+FP4X4 = mybir.dt.float4_e2m1fn_x4
+ACT = mybir.ActivationFunctionType
+ALU = mybir.AluOpType
+AX = mybir.AxisListType
+NCH = 4
+
+
+def by_rows(raw):
+    return raw[:].rearrange("p t (c i) -> p c t i", i=4)
+
+
+def by_words(bf):
+    return bf[:].rearrange("p (c i) t -> p c t i", i=4)
+
+
+def flat(bf):
+    return bf[:].rearrange("p c t -> p (c t)")
+
+
+def grouped(ap):
+    return ap.rearrange("p (g e) -> p g e", e=GROUP)
+
+
+def spread(ap):
+    return ap.unsqueeze(2).to_broadcast([P, ap.shape[1], GROUP])
+
+
+def entries(lists, cols):
+    return lists[:, cols.start // 16 : cols.stop // 16]
+
+
+def pieces(total, count):
+    width = total // count
+    return [slice(c * width, (c + 1) * width) for c in range(count)]
+
+
+def tile_attend_cpickscaled_kernel(tc, tab_words, tab_scales, w1, gain, pb, wo, dy, old, offs, offs2, out):
+    nc = tc.nc
+    with ExitStack() as ctx:
+        sb = ctx.enter_context(tc.tile_pool(name="sb", bufs=1))
+        ps = ctx.enter_context(tc.psum_pool(name="ps", bufs=1))
+
+        words = sb.tile([P, T], U16, name="words", tag="words_then_dy", align_bytes=64)
+        scales = sb.tile([P, T], U8, name="scales", tag="scales_then_wo", align_bytes=64)
+        slots = sb.tile([P, J // 16], U16, name="slots")
+        picks = sb.tile([P, M // 16], U16, name="picks")
+        w1_raw = sb.tile([P, PACK, R], F32, name="w1_raw", tag="w1_wo_s")
+        gain_sb = sb.tile([P, 1], F32, name="gain_sb")
+        pb_cols = sb.tile([P, 2], F32, name="pb_cols")
+        window = sb.tile([P, J], F32, name="window")
+        ident = sb.tile([P, P], F32, name="ident")
+
+        nc.vector.memset(scales[:].bitcast(I32), 0)
+        nc.sync.dma_start(slots[:], offs)
+        nc.sync.dma_start(picks[:], offs2)
+        nc.scalar.dma_start(out=words[:].bitcast(I32), in_=tab_words[0].bitcast(I32))
+        nc.scalar.dma_start(out=w1_raw[:], in_=w1.rearrange("(p t) r -> p t r", t=PACK))
+        nc.sync.dma_start(out=pb_cols[:], in_=pb.rearrange("o (p e) -> (o p) e", e=2))
+        nc.sync.dma_start(out=gain_sb[:], in_=gain)
+        for quad in range(4):
+            nc.sync.dma_start(
+                out=scales[32 * quad : 32 * quad + 4, :].bitcast(I32),
+                in_=tab_scales[0, 4 * quad : 4 * quad + 4, :].bitcast(I32),
+            )
+        make_identity(nc, ident[:])
+        nc.vector.memset(window[:], 0.0)
+
+        w1_bf = sb.tile([P, R, PACK], BF16, name="w1_bf", tag="w1_then_old", align_bytes=64)
+        nc.scalar.copy(out=by_words(w1_bf), in_=by_rows(w1_raw))
+        wo_raw = sb.tile([P, PACK, R], F32, name="wo_raw", tag="w1_wo_s")
+        nc.sync.dma_start(out=wo_raw[:], in_=wo.rearrange("(p t) r -> p t r", t=PACK))
+
+        g_scales = sb.tile([P, J], U8, name="g_scales", align_bytes=64)
+        g_words = sb.tile([P, J], U16, name="g_words", align_bytes=64)
+        w1_codes = sb.tile([P, R], U32, name="w1_codes", align_bytes=64)
+        w1_scales = sb.tile([P, R], U8, name="w1_scales", align_bytes=64)
+        first, second = pieces(J, 2)
+        nc.vector.tensor_copy(g_words[:], words[:].indirect(slots[:]))
+        nc.vector.tensor_copy(g_scales[:, first], scales[:].indirect(entries(slots, first)))
+        nc.vector.quantize_mx(out=w1_codes[:].bitcast(FP8X4), scales=w1_scales[:], in_=flat(w1_bf))
+        nc.vector.tensor_copy(g_scales[:, second], scales[:].indirect(entries(slots, second)))
+
+        dy_raw = sb.tile([P, PACK, M], F32, name="dy_raw", tag="words_then_dy", align_bytes=64)
+        nc.sync.dma_start(out=dy_raw[:], in_=dy.rearrange("(p t) m -> p t m", t=PACK))
+        old_sb = sb.tile([P, J], F32, name="old_sb", tag="w1_then_old", align_bytes=64)
+        nc.sync.dma_start(out=old_sb[:], in_=old)
+
+        pb_ps = ps.tile([P, 2, P], F32, name="pb_ps")
+        for e in range(2):
+            nc.tensor.transpose(pb_ps[:, e, :], pb_cols[:, e : e + 1].to_broadcast([P, P]), ident[:])
+        pb_all = sb.tile([P, M], F32, name="pb_all")
+        nc.scalar.copy(out=pb_all[:].rearrange("p (k e) -> p k e", e=2), in_=pb_ps[:].rearrange("p e k -> p k e"))
+
+        h1 = sb.tile([P, J], F32, name="h1")
+        quarters = pieces(J, 4)
+        wo_bf = sb.tile([P, R, PACK], BF16, name="wo_bf", tag="scales_then_wo", align_bytes=64)
+        for n, cols in enumerate((first, quarters[2], quarters[3])):
+            a_ps = ps.tile([P, cols.stop - cols.start], F32, name="a_ps%d" % n)
+            nc.tensor.matmul_mx(
+                out=a_ps[:], lhsT=w1_codes[:].bitcast(FP8X4), lhsT_scale=w1_scales[:],
+                rhs=g_words[:, cols].bitcast(FP4X4), rhs_scale=g_scales[:, cols], start=True, stop=True,
+            )
+            if n < 2:
+                nc.scalar.activation(out=h1[:, cols], in_=a_ps[:], func=ACT.Copy, scale=gain_sb[:])
+            else:
+                nc.vector.tensor_copy(out=by_words(wo_bf), in_=by_rows(wo_raw))
+                nc.vector.tensor_scalar_mul(h1[:, cols], a_ps[:], gain_sb[:])
+
+        s = sb.tile([P, M], F32, name="s", tag="w1_wo_s")
+        sq = sb.tile([P, M], F32, name="sq", tag="squares_then_dy", align_bytes=64)
+        ssum = sb.tile([P, G], F32, name="ssum")
+        halves = pieces(M, 2)
+        for cols in halves:
+            nc.vector.tensor_tensor(s[:, cols], h1[:].indirect(entries(picks, cols)), pb_all[:, cols], ALU.add)
+        for cols in halves:
+            nc.vector.tensor_tensor(sq[:, cols], s[:, cols], s[:, cols], ALU.mult)
+        for cols, groups in zip(halves, pieces(G, 2)):
+            nc.vector.tensor_reduce(out=ssum[:, groups], in_=grouped(sq[:, cols]), axis=AX.X, op=ALU.add)
+        rms = sb.tile([P, G], F32, name="rms")
+        nc.scalar.activation(out=rms[:], in_=ssum[:], func=ACT.Sqrt, scale=1.0 / GROUP, bias=0.1)
+
+        dy_bf = sb.tile([P, M, PACK], BF16, name="dy_bf", tag="squares_then_dy", align_bytes=64)
+        wo_codes = sb.tile([P, R], U32, name="wo_codes", align_bytes=64)
+        wo_scales = sb.tile([P, R], U8, name="wo_scales", align_bytes=64)
+        dy_codes = sb.tile([P, M], U32, name="dy_codes", align_bytes=64)
+        dy_scales = sb.tile([P, M], U8, name="dy_scales", align_bytes=64)
+        inv = sb.tile([P, G], F32, name="inv")
+        u = sb.tile([P, M], F32, name="u")
+        cn = sb.tile([P, M], F32, name="cn")
+        c0_ps = ps.tile([P, M], F32, name="c0_ps")
+        nc.vector.tensor_copy(out=by_words(dy_bf), in_=by_rows(dy_raw))
+        nc.vector.reciprocal(out=inv[:], in_=rms[:])
+        nc.vector.quantize_mx(out=dy_codes[:].bitcast(FP8X4), scales=dy_scales[:], in_=flat(dy_bf))
+        nc.vector.quantize_mx(out=wo_codes[:].bitcast(FP8X4), scales=wo_scales[:], in_=flat(wo_bf))
+        nc.vector.tensor_tensor(grouped(u[:]), grouped(s[:]), spread(inv[:]), ALU.mult)
+        nc.tensor.matmul_mx(
+            out=c0_ps[:], lhsT=wo_codes[:].bitcast(FP8X4), lhsT_scale=wo_scales[:],
+            rhs=dy_codes[:].bitcast(FP8X4), rhs_scale=dy_scales[:], start=True, stop=True,
+        )
+        nc.vector.scalar_tensor_tensor(grouped(cn[:]), grouped(c0_ps[:]), -0.5, spread(inv[:]), ALU.mult, ALU.mult)
+
+        th = sb.tile([P, M], F32, name="th")
+        sl = sb.tile([P, M], F32, name="sl")
+        half_d = sb.tile([P, M], F32, name="half_d")
+        d = sb.tile([P, M], F32, name="d")
+        du = sb.tile([P, M], F32, name="du")
+        dsum = sb.tile([P, G], F32, name="dsum")
+        corr = sb.tile([P, M], F32, name="corr")
+        chunks = pieces(M, NCH)
+        chunk_groups = pieces(G, NCH)
+        for c in chunks:
+            nc.scalar.activation(out=sl[:, c], in_=u[:, c], func=ACT.Silu, scale=-1.0)
+            nc.scalar.activation(out=th[:, c], in_=u[:, c], func=ACT.Tanh, scale=0.5)
+        for c in chunks:
+            nc.vector.scalar_tensor_tensor(half_d[:, c], th[:, c], 1.0, cn[:, c], ALU.add, ALU.mult)
+        for c in chunks:
+            nc.vector.scalar_tensor_tensor(d[:, c], sl[:, c], -1.0, half_d[:, c], ALU.add, ALU.mult)
+        for c in chunks:
+            nc.vector.tensor_tensor(du[:, c], d[:, c], u[:, c], ALU.mult)
+        for c, g in zip(chunks, chunk_groups):
+            nc.vector.tensor_reduce(out=dsum[:, g], in_=grouped(du[:, c]), axis=AX.X, op=ALU.add)
+        for c, g in zip(chunks, chunk_groups):
+            nc.vector.scalar_tensor_tensor(grouped(corr[:, c]), grouped(u[:, c]), -1.0 / GROUP, spread(dsum[:, g]), ALU.mult, ALU.mult)
+        for cols in halves:
+            nc.vector.tensor_tensor(window[:].indirect(entries(picks, cols)), d[:, cols], corr[:, cols], ALU.add)
+
+        res = sb.tile([P, J], F32, name="res")
+        for cols, queue in zip((first, second), (nc.sync, nc.scalar)):
+            nc.vector.scalar_tensor_tensor(res[:, cols], window[:, cols], gain_sb[:], old_sb[:, cols], ALU.mult, ALU.add)
+            queue.dma_start(out=out[:, cols], in_=res[:, cols])

@@ -1,7 +1,6 @@
 from contextlib import ExitStack
 
 import concourse.mybir as mybir
-from concourse.masks import make_identity
 
 K, R, F, T, J, M, G = 512, 128, 512, 2048, 512, 256, 32
 P = 128
@@ -20,11 +19,11 @@ FP4X4 = mybir.dt.float4_e2m1fn_x4
 ACT = mybir.ActivationFunctionType
 ALU = mybir.AluOpType
 AX = mybir.AxisListType
-NCH = 4
+NCH = 2
 
 
 def by_rows(raw):
-    return raw[:].rearrange("p t (c i) -> p c t i", i=4)
+    return raw.rearrange("p t (c i) -> p c t i", i=4)
 
 
 def by_words(bf):
@@ -56,15 +55,14 @@ def tile_attend_cpickscaled_kernel(tc, tab_words, tab_scales, w1, gain, pb, wo, 
     nc = tc.nc
     with ExitStack() as ctx:
         sb = ctx.enter_context(tc.tile_pool(name="sb", bufs=1))
+        mid = ctx.enter_context(tc.tile_pool(name="mid", bufs=1))
         ps = ctx.enter_context(tc.psum_pool(name="ps", bufs=1))
 
-        words = sb.tile([P, T], U16, name="words", tag="words_then_dy", align_bytes=64)
-        scales = sb.tile([P, T], U8, name="scales", tag="scales_then_wo", align_bytes=64)
+        words = sb.tile([P, T], U16, name="words", align_bytes=64)
+        scales = sb.tile([P, T], U8, name="scales", align_bytes=64)
         slots = sb.tile([P, J // 16], U16, name="slots")
         picks = sb.tile([P, M // 16], U16, name="picks")
-        w1_raw = sb.tile([P, PACK, R], F32, name="w1_raw", tag="w1_wo_s")
-        gain_sb = sb.tile([P, 1], F32, name="gain_sb")
-        pb_cols = sb.tile([P, 2], F32, name="pb_cols")
+        w1_raw = sb.tile([P, PACK, R], F32, name="w1_raw", tag="w1_then_wo")
         window = sb.tile([P, J], F32, name="window")
         ident = sb.tile([P, P], F32, name="ident")
 
@@ -73,6 +71,8 @@ def tile_attend_cpickscaled_kernel(tc, tab_words, tab_scales, w1, gain, pb, wo, 
         nc.sync.dma_start(picks[:], offs2)
         nc.scalar.dma_start(out=words[:].bitcast(I32), in_=tab_words[0].bitcast(I32))
         nc.scalar.dma_start(out=w1_raw[:], in_=w1.rearrange("(p t) r -> p t r", t=PACK))
+        gain_sb = sb.tile([P, 1], F32, name="gain_sb")
+        pb_cols = sb.tile([P, 2], F32, name="pb_cols")
         nc.sync.dma_start(out=pb_cols[:], in_=pb.rearrange("o (p e) -> (o p) e", e=2))
         nc.sync.dma_start(out=gain_sb[:], in_=gain)
         for quad in range(4):
@@ -80,16 +80,26 @@ def tile_attend_cpickscaled_kernel(tc, tab_words, tab_scales, w1, gain, pb, wo, 
                 out=scales[32 * quad : 32 * quad + 4, :].bitcast(I32),
                 in_=tab_scales[0, 4 * quad : 4 * quad + 4, :].bitcast(I32),
             )
-        make_identity(nc, ident[:])
+        warm_in = sb.tile([P, 1], F32, name="warm_in")
+        warm_sqrt = sb.tile([P, 1], F32, name="warm_sqrt")
+        nc.vector.memset(warm_in[:], 1.0)
+        nc.scalar.activation(out=warm_sqrt[:], in_=warm_in[:], func=ACT.Sqrt)
+        zeros = sb.tile([P, P], F32, name="zeros", tag="zeros_dy_rms")
         nc.vector.memset(window[:], 0.0)
+        nc.vector.memset(zeros[:], 0.0)
+        nc.gpsimd.affine_select(
+            out=ident[:], in_=zeros[:], compare_op=ALU.not_equal, fill=1.0, base=0, pattern=[[-1, P]], channel_multiplier=1
+        )
+        dy_raw = sb.tile([P, PACK, M], F32, name="dy_raw", tag="zeros_dy_rms")
+        nc.sync.dma_start(out=dy_raw[:], in_=dy.rearrange("(p t) m -> p t m", t=PACK))
 
         w1_bf = sb.tile([P, R, PACK], BF16, name="w1_bf", tag="w1_then_old", align_bytes=64)
-        nc.scalar.copy(out=by_words(w1_bf), in_=by_rows(w1_raw))
-        wo_raw = sb.tile([P, PACK, R], F32, name="wo_raw", tag="w1_wo_s")
-        nc.sync.dma_start(out=wo_raw[:], in_=wo.rearrange("(p t) r -> p t r", t=PACK))
+        nc.scalar.copy(out=by_words(w1_bf), in_=by_rows(w1_raw[:]))
 
+        wo_raw = sb.tile([P, PACK, R], F32, name="wo_raw", tag="w1_then_wo")
+        nc.sync.dma_start(out=wo_raw[:], in_=wo.rearrange("(p t) r -> p t r", t=PACK))
         g_scales = sb.tile([P, J], U8, name="g_scales", align_bytes=64)
-        g_words = sb.tile([P, J], U16, name="g_words", align_bytes=64)
+        g_words = sb.tile([P, J], U16, name="g_words", tag="gathered_then_dy", align_bytes=64)
         w1_codes = sb.tile([P, R], U32, name="w1_codes", align_bytes=64)
         w1_scales = sb.tile([P, R], U8, name="w1_scales", align_bytes=64)
         first, second = pieces(J, 2)
@@ -98,8 +108,6 @@ def tile_attend_cpickscaled_kernel(tc, tab_words, tab_scales, w1, gain, pb, wo, 
         nc.vector.quantize_mx(out=w1_codes[:].bitcast(FP8X4), scales=w1_scales[:], in_=flat(w1_bf))
         nc.vector.tensor_copy(g_scales[:, second], scales[:].indirect(entries(slots, second)))
 
-        dy_raw = sb.tile([P, PACK, M], F32, name="dy_raw", tag="words_then_dy", align_bytes=64)
-        nc.sync.dma_start(out=dy_raw[:], in_=dy.rearrange("(p t) m -> p t m", t=PACK))
         old_sb = sb.tile([P, J], F32, name="old_sb", tag="w1_then_old", align_bytes=64)
         nc.sync.dma_start(out=old_sb[:], in_=old)
 
@@ -111,7 +119,6 @@ def tile_attend_cpickscaled_kernel(tc, tab_words, tab_scales, w1, gain, pb, wo, 
 
         h1 = sb.tile([P, J], F32, name="h1")
         quarters = pieces(J, 4)
-        wo_bf = sb.tile([P, R, PACK], BF16, name="wo_bf", tag="scales_then_wo", align_bytes=64)
         for n, cols in enumerate((first, quarters[2], quarters[3])):
             a_ps = ps.tile([P, cols.stop - cols.start], F32, name="a_ps%d" % n)
             nc.tensor.matmul_mx(
@@ -121,11 +128,13 @@ def tile_attend_cpickscaled_kernel(tc, tab_words, tab_scales, w1, gain, pb, wo, 
             if n < 2:
                 nc.scalar.activation(out=h1[:, cols], in_=a_ps[:], func=ACT.Copy, scale=gain_sb[:])
             else:
-                nc.vector.tensor_copy(out=by_words(wo_bf), in_=by_rows(wo_raw))
                 nc.vector.tensor_scalar_mul(h1[:, cols], a_ps[:], gain_sb[:])
 
-        s = sb.tile([P, M], F32, name="s", tag="w1_wo_s")
-        sq = sb.tile([P, M], F32, name="sq", tag="squares_then_dy", align_bytes=64)
+        dy_bf = sb.tile([P, M, PACK], BF16, name="dy_bf", tag="gathered_then_dy", align_bytes=64)
+        nc.scalar.copy(out=by_words(dy_bf), in_=by_rows(dy_raw[:]))
+
+        s = sb.tile([P, M], F32, name="s")
+        sq = mid.tile([P, M], F32, name="sq", offset=512, align_bytes=64)
         ssum = sb.tile([P, G], F32, name="ssum")
         halves = pieces(M, 2)
         for cols in halves:
@@ -134,21 +143,21 @@ def tile_attend_cpickscaled_kernel(tc, tab_words, tab_scales, w1, gain, pb, wo, 
             nc.vector.tensor_tensor(sq[:, cols], s[:, cols], s[:, cols], ALU.mult)
         for cols, groups in zip(halves, pieces(G, 2)):
             nc.vector.tensor_reduce(out=ssum[:, groups], in_=grouped(sq[:, cols]), axis=AX.X, op=ALU.add)
-        rms = sb.tile([P, G], F32, name="rms")
+        rms = sb.tile([P, G], F32, name="rms", tag="zeros_dy_rms")
         nc.scalar.activation(out=rms[:], in_=ssum[:], func=ACT.Sqrt, scale=1.0 / GROUP, bias=0.1)
 
-        dy_bf = sb.tile([P, M, PACK], BF16, name="dy_bf", tag="squares_then_dy", align_bytes=64)
         wo_codes = sb.tile([P, R], U32, name="wo_codes", align_bytes=64)
         wo_scales = sb.tile([P, R], U8, name="wo_scales", align_bytes=64)
-        dy_codes = sb.tile([P, M], U32, name="dy_codes", align_bytes=64)
+        dy_codes = mid.tile([P, M], U32, name="dy_codes", offset=0, align_bytes=64)
+        wo_bf = mid.tile([P, R, PACK], BF16, name="wo_bf", offset=1024, align_bytes=64)
         dy_scales = sb.tile([P, M], U8, name="dy_scales", align_bytes=64)
         inv = sb.tile([P, G], F32, name="inv")
         u = sb.tile([P, M], F32, name="u")
         cn = sb.tile([P, M], F32, name="cn")
         c0_ps = ps.tile([P, M], F32, name="c0_ps")
-        nc.vector.tensor_copy(out=by_words(dy_bf), in_=by_rows(dy_raw))
-        nc.vector.reciprocal(out=inv[:], in_=rms[:])
+        nc.vector.tensor_copy(out=by_words(wo_bf), in_=by_rows(wo_raw[:]))
         nc.vector.quantize_mx(out=dy_codes[:].bitcast(FP8X4), scales=dy_scales[:], in_=flat(dy_bf))
+        nc.vector.reciprocal(out=inv[:], in_=rms[:])
         nc.vector.quantize_mx(out=wo_codes[:].bitcast(FP8X4), scales=wo_scales[:], in_=flat(wo_bf))
         nc.vector.tensor_tensor(grouped(u[:]), grouped(s[:]), spread(inv[:]), ALU.mult)
         nc.tensor.matmul_mx(
@@ -169,14 +178,16 @@ def tile_attend_cpickscaled_kernel(tc, tab_words, tab_scales, w1, gain, pb, wo, 
         for c in chunks:
             nc.scalar.activation(out=sl[:, c], in_=u[:, c], func=ACT.Silu, scale=-1.0)
             nc.scalar.activation(out=th[:, c], in_=u[:, c], func=ACT.Tanh, scale=0.5)
+        slu = sb.tile([P, M], F32, name="slu")
         for c in chunks:
+            nc.vector.scalar_tensor_tensor(slu[:, c], sl[:, c], -1.0, u[:, c], ALU.add, ALU.mult)
             nc.vector.scalar_tensor_tensor(half_d[:, c], th[:, c], 1.0, cn[:, c], ALU.add, ALU.mult)
         for c in chunks:
-            nc.vector.scalar_tensor_tensor(d[:, c], sl[:, c], -1.0, half_d[:, c], ALU.add, ALU.mult)
-        for c in chunks:
-            nc.vector.tensor_tensor(du[:, c], d[:, c], u[:, c], ALU.mult)
+            nc.vector.tensor_tensor(du[:, c], half_d[:, c], slu[:, c], ALU.mult)
         for c, g in zip(chunks, chunk_groups):
             nc.vector.tensor_reduce(out=dsum[:, g], in_=grouped(du[:, c]), axis=AX.X, op=ALU.add)
+        for c in chunks:
+            nc.vector.scalar_tensor_tensor(d[:, c], sl[:, c], -1.0, half_d[:, c], ALU.add, ALU.mult)
         for c, g in zip(chunks, chunk_groups):
             nc.vector.scalar_tensor_tensor(grouped(corr[:, c]), grouped(u[:, c]), -1.0 / GROUP, spread(dsum[:, g]), ALU.mult, ALU.mult)
         for cols in halves:

@@ -69,8 +69,8 @@ def tile_attend_cpickscaled_kernel(tc, tab_words, tab_scales, w1, gain, pb, wo, 
         nc.vector.memset(scales[:].bitcast(I32), 0)
         nc.sync.dma_start(slots[:], offs)
         nc.sync.dma_start(picks[:], offs2)
-        nc.scalar.dma_start(out=words[:].bitcast(I32), in_=tab_words[0].bitcast(I32))
-        nc.scalar.dma_start(out=w1_raw[:], in_=w1.rearrange("(p t) r -> p t r", t=PACK))
+        nc.sync.dma_start(out=words[:].bitcast(I32), in_=tab_words[0].bitcast(I32))
+        nc.sync.dma_start(out=w1_raw[:], in_=w1.rearrange("(p t) r -> p t r", t=PACK))
         gain_sb = sb.tile([P, 1], F32, name="gain_sb")
         pb_cols = sb.tile([P, 2], F32, name="pb_cols")
         nc.sync.dma_start(out=pb_cols[:], in_=pb.rearrange("o (p e) -> (o p) e", e=2))

@@ -67,14 +67,14 @@ def tile_attend_cpickscaled_kernel(tc, tab_words, tab_scales, w1, gain, pb, wo, 
         ident = sb.tile([P, P], F32, name="ident")
 
         nc.vector.memset(scales[:].bitcast(I32), 0)
-        nc.sync.dma_start(slots[:], offs)
-        nc.sync.dma_start(picks[:], offs2)
         nc.sync.dma_start(out=words[:].bitcast(I32), in_=tab_words[0].bitcast(I32))
+        nc.sync.dma_start(slots[:], offs)
         nc.sync.dma_start(out=w1_raw[:], in_=w1.rearrange("(p t) r -> p t r", t=PACK))
+        nc.sync.dma_start(picks[:], offs2)
         gain_sb = sb.tile([P, 1], F32, name="gain_sb")
         pb_cols = sb.tile([P, 2], F32, name="pb_cols")
-        nc.sync.dma_start(out=pb_cols[:], in_=pb.rearrange("o (p e) -> (o p) e", e=2))
-        nc.sync.dma_start(out=gain_sb[:], in_=gain)
+        nc.gpsimd.dma_start(out=pb_cols[:], in_=pb.rearrange("o (p e) -> (o p) e", e=2))
+        nc.gpsimd.dma_start(out=gain_sb[:], in_=gain)
         for quad in range(4):
             nc.sync.dma_start(
                 out=scales[32 * quad : 32 * quad + 4, :].bitcast(I32),

from contextlib import ExitStack

import concourse.mybir as mybir

K, R, F, T, J, M, G = 512, 128, 512, 2048, 512, 256, 32
P = 128
PACK = 4
GROUP = M // G
FLOPS = 2 * K * R * J + 2 * F * R * M

F32 = mybir.dt.float32
BF16 = mybir.dt.bfloat16
I32 = mybir.dt.int32
U32 = mybir.dt.uint32
U16 = mybir.dt.uint16
U8 = mybir.dt.uint8
FP8X4 = mybir.dt.float8_e4m3fn_x4
FP4X4 = mybir.dt.float4_e2m1fn_x4
ACT = mybir.ActivationFunctionType
ALU = mybir.AluOpType
AX = mybir.AxisListType
NCH = 2


def by_rows(raw):
    return raw.rearrange("p t (c i) -> p c t i", i=4)


def by_words(bf):
    return bf[:].rearrange("p (c i) t -> p c t i", i=4)


def flat(bf):
    return bf[:].rearrange("p c t -> p (c t)")


def grouped(ap):
    return ap.rearrange("p (g e) -> p g e", e=GROUP)


def spread(ap):
    return ap.unsqueeze(2).to_broadcast([P, ap.shape[1], GROUP])


def entries(lists, cols):
    return lists[:, cols.start // 16 : cols.stop // 16]


def pieces(total, count):
    width = total // count
    return [slice(c * width, (c + 1) * width) for c in range(count)]


def tile_attend_cpickscaled_kernel(tc, tab_words, tab_scales, w1, gain, pb, wo, dy, old, offs, offs2, out):
    nc = tc.nc
    with ExitStack() as ctx:
        sb = ctx.enter_context(tc.tile_pool(name="sb", bufs=1))
        mid = ctx.enter_context(tc.tile_pool(name="mid", bufs=1))
        ps = ctx.enter_context(tc.psum_pool(name="ps", bufs=1))

        words = sb.tile([P, T], U16, name="words", align_bytes=64)
        scales = sb.tile([P, T], U8, name="scales", align_bytes=64)
        slots = sb.tile([P, J // 16], U16, name="slots")
        picks = sb.tile([P, M // 16], U16, name="picks")
        w1_raw = sb.tile([P, PACK, R], F32, name="w1_raw", tag="w1_then_wo")
        window = sb.tile([P, J], F32, name="window")
        ident = sb.tile([P, P], F32, name="ident")

        nc.vector.memset(scales[:].bitcast(I32), 0)
        nc.sync.dma_start(out=words[:].bitcast(I32), in_=tab_words[0].bitcast(I32))
        nc.sync.dma_start(slots[:], offs)
        nc.sync.dma_start(out=w1_raw[:], in_=w1.rearrange("(p t) r -> p t r", t=PACK))
        nc.sync.dma_start(picks[:], offs2)
        gain_sb = sb.tile([P, 1], F32, name="gain_sb")
        pb_cols = sb.tile([P, 2], F32, name="pb_cols")
        nc.gpsimd.dma_start(out=pb_cols[:], in_=pb.rearrange("o (p e) -> (o p) e", e=2))
        nc.gpsimd.dma_start(out=gain_sb[:], in_=gain)
        for quad in range(4):
            nc.sync.dma_start(
                out=scales[32 * quad : 32 * quad + 4, :].bitcast(I32),
                in_=tab_scales[0, 4 * quad : 4 * quad + 4, :].bitcast(I32),
            )
        warm_in = sb.tile([P, 1], F32, name="warm_in")
        warm_sqrt = sb.tile([P, 1], F32, name="warm_sqrt")
        nc.vector.memset(warm_in[:], 1.0)
        nc.scalar.activation(out=warm_sqrt[:], in_=warm_in[:], func=ACT.Sqrt)
        zeros = sb.tile([P, P], F32, name="zeros", tag="zeros_dy_rms")
        nc.vector.memset(window[:], 0.0)
        nc.vector.memset(zeros[:], 0.0)
        nc.gpsimd.affine_select(
            out=ident[:], in_=zeros[:], compare_op=ALU.not_equal, fill=1.0, base=0, pattern=[[-1, P]], channel_multiplier=1
        )
        dy_raw = sb.tile([P, PACK, M], F32, name="dy_raw", tag="zeros_dy_rms")
        nc.sync.dma_start(out=dy_raw[:], in_=dy.rearrange("(p t) m -> p t m", t=PACK))

        w1_bf = sb.tile([P, R, PACK], BF16, name="w1_bf", tag="w1_then_old", align_bytes=64)
        nc.scalar.copy(out=by_words(w1_bf), in_=by_rows(w1_raw[:]))

        wo_raw = sb.tile([P, PACK, R], F32, name="wo_raw", tag="w1_then_wo")
        nc.sync.dma_start(out=wo_raw[:], in_=wo.rearrange("(p t) r -> p t r", t=PACK))
        g_scales = sb.tile([P, J], U8, name="g_scales", align_bytes=64)
        g_words = sb.tile([P, J], U16, name="g_words", tag="gathered_then_dy", align_bytes=64)
        w1_codes = sb.tile([P, R], U32, name="w1_codes", align_bytes=64)
        w1_scales = sb.tile([P, R], U8, name="w1_scales", align_bytes=64)
        first, second = pieces(J, 2)
        nc.vector.tensor_copy(g_words[:], words[:].indirect(slots[:]))
        nc.vector.tensor_copy(g_scales[:, first], scales[:].indirect(entries(slots, first)))
        nc.vector.quantize_mx(out=w1_codes[:].bitcast(FP8X4), scales=w1_scales[:], in_=flat(w1_bf))
        nc.vector.tensor_copy(g_scales[:, second], scales[:].indirect(entries(slots, second)))

        old_sb = sb.tile([P, J], F32, name="old_sb", tag="w1_then_old", align_bytes=64)
        nc.sync.dma_start(out=old_sb[:], in_=old)

        pb_ps = ps.tile([P, 2, P], F32, name="pb_ps")
        for e in range(2):
            nc.tensor.transpose(pb_ps[:, e, :], pb_cols[:, e : e + 1].to_broadcast([P, P]), ident[:])
        pb_all = sb.tile([P, M], F32, name="pb_all")
        nc.scalar.copy(out=pb_all[:].rearrange("p (k e) -> p k e", e=2), in_=pb_ps[:].rearrange("p e k -> p k e"))

        h1 = sb.tile([P, J], F32, name="h1")
        quarters = pieces(J, 4)
        for n, cols in enumerate((first, quarters[2], quarters[3])):
            a_ps = ps.tile([P, cols.stop - cols.start], F32, name="a_ps%d" % n)
            nc.tensor.matmul_mx(
                out=a_ps[:], lhsT=w1_codes[:].bitcast(FP8X4), lhsT_scale=w1_scales[:],
                rhs=g_words[:, cols].bitcast(FP4X4), rhs_scale=g_scales[:, cols], start=True, stop=True,
            )
            if n < 2:
                nc.scalar.activation(out=h1[:, cols], in_=a_ps[:], func=ACT.Copy, scale=gain_sb[:])
            else:
                nc.vector.tensor_scalar_mul(h1[:, cols], a_ps[:], gain_sb[:])

        dy_bf = sb.tile([P, M, PACK], BF16, name="dy_bf", tag="gathered_then_dy", align_bytes=64)
        nc.scalar.copy(out=by_words(dy_bf), in_=by_rows(dy_raw[:]))

        s = sb.tile([P, M], F32, name="s")
        sq = mid.tile([P, M], F32, name="sq", offset=512, align_bytes=64)
        ssum = sb.tile([P, G], F32, name="ssum")
        halves = pieces(M, 2)
        for cols in halves:
            nc.vector.tensor_tensor(s[:, cols], h1[:].indirect(entries(picks, cols)), pb_all[:, cols], ALU.add)
        for cols in halves:
            nc.vector.tensor_tensor(sq[:, cols], s[:, cols], s[:, cols], ALU.mult)
        for cols, groups in zip(halves, pieces(G, 2)):
            nc.vector.tensor_reduce(out=ssum[:, groups], in_=grouped(sq[:, cols]), axis=AX.X, op=ALU.add)
        rms = sb.tile([P, G], F32, name="rms", tag="zeros_dy_rms")
        nc.scalar.activation(out=rms[:], in_=ssum[:], func=ACT.Sqrt, scale=1.0 / GROUP, bias=0.1)

        wo_codes = sb.tile([P, R], U32, name="wo_codes", align_bytes=64)
        wo_scales = sb.tile([P, R], U8, name="wo_scales", align_bytes=64)
        dy_codes = mid.tile([P, M], U32, name="dy_codes", offset=0, align_bytes=64)
        wo_bf = mid.tile([P, R, PACK], BF16, name="wo_bf", offset=1024, align_bytes=64)
        dy_scales = sb.tile([P, M], U8, name="dy_scales", align_bytes=64)
        inv = sb.tile([P, G], F32, name="inv")
        u = sb.tile([P, M], F32, name="u")
        cn = sb.tile([P, M], F32, name="cn")
        c0_ps = ps.tile([P, M], F32, name="c0_ps")
        nc.vector.tensor_copy(out=by_words(wo_bf), in_=by_rows(wo_raw[:]))
        nc.vector.quantize_mx(out=dy_codes[:].bitcast(FP8X4), scales=dy_scales[:], in_=flat(dy_bf))
        nc.vector.reciprocal(out=inv[:], in_=rms[:])
        nc.vector.quantize_mx(out=wo_codes[:].bitcast(FP8X4), scales=wo_scales[:], in_=flat(wo_bf))
        nc.vector.tensor_tensor(grouped(u[:]), grouped(s[:]), spread(inv[:]), ALU.mult)
        nc.tensor.matmul_mx(
            out=c0_ps[:], lhsT=wo_codes[:].bitcast(FP8X4), lhsT_scale=wo_scales[:],
            rhs=dy_codes[:].bitcast(FP8X4), rhs_scale=dy_scales[:], start=True, stop=True,
        )
        nc.vector.scalar_tensor_tensor(grouped(cn[:]), grouped(c0_ps[:]), -0.5, spread(inv[:]), ALU.mult, ALU.mult)

        th = sb.tile([P, M], F32, name="th")
        sl = sb.tile([P, M], F32, name="sl")
        half_d = sb.tile([P, M], F32, name="half_d")
        d = sb.tile([P, M], F32, name="d")
        du = sb.tile([P, M], F32, name="du")
        dsum = sb.tile([P, G], F32, name="dsum")
        corr = sb.tile([P, M], F32, name="corr")
        chunks = pieces(M, NCH)
        chunk_groups = pieces(G, NCH)
        for c in chunks:
            nc.scalar.activation(out=sl[:, c], in_=u[:, c], func=ACT.Silu, scale=-1.0)
            nc.scalar.activation(out=th[:, c], in_=u[:, c], func=ACT.Tanh, scale=0.5)
        slu = sb.tile([P, M], F32, name="slu")
        for c in chunks:
            nc.vector.scalar_tensor_tensor(slu[:, c], sl[:, c], -1.0, u[:, c], ALU.add, ALU.mult)
            nc.vector.scalar_tensor_tensor(half_d[:, c], th[:, c], 1.0, cn[:, c], ALU.add, ALU.mult)
        for c in chunks:
            nc.vector.tensor_tensor(du[:, c], half_d[:, c], slu[:, c], ALU.mult)
        for c, g in zip(chunks, chunk_groups):
            nc.vector.tensor_reduce(out=dsum[:, g], in_=grouped(du[:, c]), axis=AX.X, op=ALU.add)
        for c in chunks:
            nc.vector.scalar_tensor_tensor(d[:, c], sl[:, c], -1.0, half_d[:, c], ALU.add, ALU.mult)
        for c, g in zip(chunks, chunk_groups):
            nc.vector.scalar_tensor_tensor(grouped(corr[:, c]), grouped(u[:, c]), -1.0 / GROUP, spread(dsum[:, g]), ALU.mult, ALU.mult)
        for cols in halves:
            nc.vector.tensor_tensor(window[:].indirect(entries(picks, cols)), d[:, cols], corr[:, cols], ALU.add)

        res = sb.tile([P, J], F32, name="res")
        for cols, queue in zip((first, second), (nc.sync, nc.scalar)):
            nc.vector.scalar_tensor_tensor(res[:, cols], window[:, cols], gain_sb[:], old_sb[:, cols], ALU.mult, ALU.add)
            queue.dma_start(out=out[:, cols], in_=res[:, cols])
